import numpy as np
import ml_dtypes


def mxq(x, axis, fmt="e4m3"):
    dtype, down = {"e4m3": (ml_dtypes.float8_e4m3fn, 7), "e5m2": (ml_dtypes.float8_e5m2, 14)}[fmt]
    v = np.moveaxis(np.asarray(x, np.float32).astype(ml_dtypes.bfloat16).astype(np.float64), axis, -1)
    blocks = v.reshape(v.shape[:-1] + (-1, 32))
    amax = np.abs(blocks).max(-1, keepdims=True)
    byte = np.maximum(np.where(amax > 0, np.frexp(amax)[1] - 1 + 127, 0) - down, 1)
    scale = np.exp2(byte - 127.0)
    codes = (blocks / scale).astype(np.float32).astype(dtype).astype(np.float64)
    return np.moveaxis((codes * scale).reshape(v.shape), -1, axis)


WIDE = False


def mx_kscale(k):
    if not WIDE:
        return np.ones(k)
    levels = np.array([10, -10, 5, -5, 0])
    if k % 512:
        return np.exp2(np.random.permutation(np.resize(levels, k // 32))).repeat(32)
    a = np.empty((k // 512, 16))
    for p in range(k // 512):
        a[p, :8] = np.random.permutation(np.resize(levels, 8))
        for g in range(8):
            far = levels[np.abs(levels - a[p, g]) >= 10]
            a[p, g + 8] = far[np.random.randint(len(far))]
    return np.exp2(a.ravel()).repeat(32)


def f64(x):
    return np.asarray(x).astype(np.float64)


def striped(idx):
    return np.tile(np.asarray(idx).reshape(-1, 16).T, (8, 1)).astype(np.uint16)


def unstriped(offs):
    return offs[:16].T.reshape(-1).astype(np.int64)


E2M1 = np.array([0.0, 0.5, 1.0, 1.5, 2.0, 3.0, 4.0, 6.0, -0.0, -0.5, -1.0, -1.5, -2.0, -3.0, -4.0, -6.0])


def pack_weight(w, fmt):
    k, n = w.shape
    w = f64(np.asarray(w, np.float32).astype(ml_dtypes.bfloat16)).reshape(k // 32, 32, n)
    amax = np.abs(w).max(1)
    if fmt == "e4m3":
        byte = np.frexp(amax)[1] - 1 + 127 - 7
    else:
        mant, ex = np.frexp(amax / 6.0)
        byte = np.where(mant > 0.5, ex, ex - 1) + 127
    byte = np.clip(np.where(amax > 0, byte, 1), 1, 254)
    scaled = (w * np.exp2(127.0 - byte)[:, None, :]).reshape(k, n).astype(np.float32)
    by_word = np.ascontiguousarray(scaled.reshape(k // 512, 128, 4, n).transpose(0, 1, 3, 2))
    if fmt == "e4m3":
        words = by_word.astype(ml_dtypes.float8_e4m3fn).view(np.uint8)
    else:
        c = by_word.astype(ml_dtypes.float4_e2m1fn).view(np.uint8) & 0xF
        words = (c[..., 0::2] | (c[..., 1::2] << 4)).reshape(k // 512, 128, 2 * n)
    return np.ascontiguousarray(words), np.ascontiguousarray(byte.astype(np.uint8).reshape(k // 512, 16, n))


def unpack_weight(words, scales, fmt):
    g, _, n = scales.shape
    words = np.ascontiguousarray(words).reshape(g, 128, n, -1)
    if fmt == "e4m3":
        vals = words.view(ml_dtypes.float8_e4m3fn).astype(np.float64)
    else:
        nib = np.empty((g, 128, n, 4), np.uint8)
        nib[..., 0::2] = words & 0xF
        nib[..., 1::2] = words >> 4
        vals = E2M1[nib]
    vals = vals * np.repeat(np.exp2(scales.astype(np.float64) - 127.0), 8, axis=1)[..., None]
    return vals.transpose(0, 1, 3, 2).reshape(g * 512, n)


def bf(x):
    return np.asarray(x, np.float32).astype(ml_dtypes.bfloat16)


def planes(Y):
    r, m = Y.shape
    b = f64(bf(Y)).reshape(r // 32, 32, m)
    amax = np.abs(b).max(1)
    byte = np.clip(np.where(amax > 0, np.frexp(amax)[1] - 1 + 127 - 7, 1), 1, 254)
    codes = (b * np.exp2(127.0 - byte)[:, None, :]).reshape(r, m).astype(np.float32).astype(ml_dtypes.float8_e4m3fn).view(np.uint8)
    words = codes.reshape(r // 512, 128, 4, m).transpose(0, 1, 3, 2)
    return np.ascontiguousarray(words), np.ascontiguousarray(byte.astype(np.uint8).reshape(r // 512, 16, m))


D, E, T, I, Q, U = 512, 512, 2048, 512, 256, 512


def setup_inputs():
    n = np.random.standard_normal
    idx = np.random.permutation(T)[:I]
    idx2 = np.random.randint(0, U, I)
    fd = mx_kscale(D)
    fe = mx_kscale(E)
    fi = mx_kscale(I)
    ti = np.ones(T)
    ti[idx] = fi
    keysp = pack_weight(n((D, T)) / fd[:, None], "e2m1")
    valsp = pack_weight(n((E, T)) / fe[:, None], "e2m1")
    return {
        "query": (n((D, Q)) * 0.25 / np.sqrt(D) * fd[:, None]).astype(np.float32),
        "keys_words": keysp[0],
        "keys_scales": keysp[1],
        "pquery": (n((D, Q)) * 0.4 / np.sqrt(D) * fd[:, None]).astype(np.float32),
        "place": (n((D, U)) / fd[:, None]).astype(np.float32),
        "gout": (n((E, Q)) * 1 / np.sqrt(E) * fe[:, None]).astype(np.float32),
        "vals_words": valsp[0],
        "vals_scales": valsp[1],
        "lse": (np.random.uniform(6.2, 6.5, (Q, 1))).astype(np.float32),
        "delta": (np.random.uniform(-0.3, 0.3, (Q, 1))).astype(np.float32),
        "fs": (np.random.uniform(128.0, 512.0, (1, I)) * fi).astype(np.float32),
        "keyrows": (n((D, T)) / ti).astype(np.float32),
        "res": (n((D, Q)) * 4.0).astype(np.float32),
        "offs": striped(idx),
        "offs2": striped(idx2),
    }


def reference(query, keys_words, keys_scales, pquery, place, gout, vals_words, vals_scales, lse, delta, fs, keyrows, res, offs, offs2):
    idx = unstriped(offs)
    idx2 = unstriped(offs2)
    keysu = unpack_weight(keys_words, keys_scales, "e2m1")
    valsu = unpack_weight(vals_words, vals_scales, "e2m1")
    queryq = mxq(f64(query), 0, "e4m3")
    keysidxg = keysu[:, idx]
    a = queryq.T @ keysidxg
    pqueryq = mxq(f64(pquery), 0, "e4m3")
    placeq = mxq(f64(place), 0, "e4m3")
    b = pqueryq.T @ placeq
    k1 = b[:, idx2] + 1.0
    goutq = mxq(f64(gout), 0, "e4m3")
    valsidxg = valsu[:, idx]
    dp = goutq.T @ valsidxg
    ds = np.exp(a * k1 - f64(lse)) * (dp - f64(delta)) * k1 * f64(fs)
    dt = ds.T
    kt = f64(keyrows)[:, idx].T
    ktq = mxq(kt, 0, "e4m3")
    dtq = mxq(dt, 0, "e4m3")
    gq = ktq.T @ dtq
    y = gq + f64(res)
    words, scales = planes(y)
    return y, words, scales

@@ -1,0 +1,221 @@
+from contextlib import ExitStack
+
+import concourse.mybir as mybir
+from concourse.masks import make_identity
+
+D, E, T, I, Q, U = 512, 512, 2048, 512, 256, 512
+FLOPS = 2 * Q * (D * I + D * U + E * I + I * D)
+
+F32 = mybir.dt.float32
+BF16 = mybir.dt.bfloat16
+I32 = mybir.dt.int32
+U32 = mybir.dt.uint32
+U16 = mybir.dt.uint16
+U8 = mybir.dt.uint8
+FP8X4 = mybir.dt.float8_e4m3fn_x4
+FP4X4 = mybir.dt.float4_e2m1fn_x4
+COPY = mybir.ActivationFunctionType.Copy
+EXP = mybir.ActivationFunctionType.Exp
+MULT = mybir.AluOpType.mult
+ADD = mybir.AluOpType.add
+SUB = mybir.AluOpType.subtract
+
+P = 128
+PACK = 4
+LINE = 4
+Q_TILES = Q // P
+HALF = I // 2
+LIST_HALF = HALF // 16
+
+
+def weave_views(raw, grouped, c0, c1):
+    src = raw[:, :, c0:c1].rearrange("p t (c i) -> p c t i", i=LINE)
+    dst = grouped[:, c0:c1, :].rearrange("p (c i) t -> p c t i", i=LINE)
+    return dst, src
+
+
+def tile_attend_gscaledquery_pl_kernel(tc, query, keys_words, keys_scales, pquery, place, gout, vals_words, vals_scales,
+                                        lse, delta, fs, keyrows, res, offs, offs2, out_0, out_1, out_2):
+    nc = tc.nc
+    with ExitStack() as ctx:
+        sb = ctx.enter_context(tc.tile_pool(name="sb", bufs=1))
+        ps = ctx.enter_context(tc.psum_pool(name="ps", bufs=1))
+
+        def tile(name, shape, dtype):
+            return sb.tile(shape, dtype, name=name, align_bytes=64)
+
+        def bank(name, tag, shape):
+            return ps.tile(shape, F32, name=name, tag=tag)
+
+        def load_rows(name, src):
+            raw = tile(name, [P, PACK, src.shape[1]], F32)
+            nc.sync.dma_start(out=raw[:], in_=src.rearrange("(p t) w -> p t w", t=PACK))
+            return raw
+
+        def load_packed(name, words, scales, zeroed):
+            pool_words = tile(name + "_words", [P, T], U16)
+            nc.sync.dma_start(out=pool_words[:].bitcast(I32), in_=words[0].bitcast(I32))
+            for quad in range(4):
+                nc.sync.dma_start(out=zeroed[32 * quad : 32 * quad + 4, :].bitcast(I32),
+                                  in_=scales[0, 4 * quad : 4 * quad + 4, :].bitcast(I32))
+            return pool_words
+
+        def gather_packed(name, pool_words, pool_scales):
+            words = tile(name + "_picked_words", [P, I], U16)
+            scales = tile(name + "_picked_scales", [P, I], U8)
+            nc.vector.tensor_copy(out=words[:], in_=pool_words[:].indirect(slot_list[:]))
+            nc.vector.tensor_copy(out=scales[:], in_=pool_scales[:].indirect(slot_list[:]))
+            return words, scales
+
+        def quantize(name, grouped):
+            width = grouped.shape[1]
+            codes = tile(name + "_codes", [P, width], U32)
+            scales = tile(name + "_scales", [P, width], U8)
+            nc.vector.quantize_mx(out=codes[:].bitcast(FP8X4), scales=scales[:], in_=grouped[:].rearrange("p c t -> p (c t)"))
+            return codes, scales
+
+        def product(out, stationary, cols, moving, moving_dtype):
+            nc.tensor.matmul_mx(out=out, lhsT=stationary[0][:, cols].bitcast(FP8X4), lhsT_scale=stationary[1][:, cols],
+                                rhs=moving[0][:].bitcast(moving_dtype), rhs_scale=moving[1][:], start=True, stop=True)
+
+        def turn_words(dst, rows):
+            words = rows.bitcast(F32)
+            for u in range(2):
+                nc.tensor.transpose(dst[:, u, :], words[:, u::2], ident[:])
+
+        key_scale_pool = tile("key_scale_pool", [P, T], U8)
+        val_scale_pool = tile("val_scale_pool", [P, T], U8)
+        nc.vector.memset(key_scale_pool[:].bitcast(I32), 0)
+        nc.vector.memset(val_scale_pool[:].bitcast(I32), 0)
+        ident = tile("ident", [P, P], F32)
+        make_identity(nc, ident[:])
+
+        slot_list = tile("slot_list", [P, I // 16], U16)
+        nc.sync.dma_start(slot_list[:], offs)
+        key_word_pool = load_packed("key", keys_words, keys_scales, key_scale_pool)
+        pquery_raw = load_rows("pquery_raw", pquery)
+        place_raw = load_rows("place_raw", place)
+        place_list = tile("place_list", [P, I // 16], U16)
+        nc.sync.dma_start(place_list[:], offs2)
+        val_word_pool = load_packed("val", vals_words, vals_scales, val_scale_pool)
+        query_raw = load_rows("query_raw", query)
+        lse_cols = tile("lse_cols", [P, Q_TILES], F32)
+        delta_cols = tile("delta_cols", [P, Q_TILES], F32)
+        with nc.allow_non_contiguous_dma(reason="one value a query row, on the row's partition"):
+            nc.sync.dma_start(out=lse_cols[:], in_=lse.rearrange("(m p) o -> p (m o)", p=P))
+            nc.sync.dma_start(out=delta_cols[:], in_=delta.rearrange("(m p) o -> p (m o)", p=P))
+        fs_cols = tile("fs_cols", [P, PACK], F32)
+        nc.sync.dma_start(out=fs_cols[:], in_=fs.rearrange("o (p t) -> p (o t)", t=PACK))
+        gout_raw = load_rows("gout_raw", gout)
+        keyrow_planes = keyrows.rearrange("(p j) t -> j p t", j=PACK)
+        keyrow_pool = []
+        for j in range(PACK):
+            plane = tile("keyrow_pool%d" % j, [P, T], F32)
+            nc.sync.dma_start(out=plane[:], in_=keyrow_planes[j])
+            keyrow_pool.append(plane)
+        res_raw = load_rows("res_raw", res)
+
+        keys_mx = gather_packed("key", key_word_pool, key_scale_pool)
+
+        pquery_bf = tile("pquery_bf", [P, Q, PACK], BF16)
+        nc.vector.tensor_copy(*weave_views(pquery_raw, pquery_bf, 0, Q))
+        pquery_mx = quantize("pquery", pquery_bf)
+        place_bf = tile("place_bf", [P, U, PACK], BF16)
+        split = 192
+        dst, src = weave_views(place_raw, place_bf, 0, split)
+        nc.scalar.activation(dst, src, COPY)
+        nc.vector.tensor_copy(*weave_views(place_raw, place_bf, split, U))
+        place_mx = quantize("place", place_bf)
+
+        b_banks = []
+        for m in range(Q_TILES):
+            b_bank = bank("b_bank%d" % m, "bank_b%d" % m, [P, U])
+            product(b_bank[:], pquery_mx, slice(m * P, (m + 1) * P), place_mx, FP8X4)
+            b_banks.append(b_bank)
+
+        vals_mx = gather_packed("val", val_word_pool, val_scale_pool)
+
+        query_bf = tile("query_bf", [P, Q, PACK], BF16)
+        dst, src = weave_views(query_raw, query_bf, 0, Q)
+        nc.scalar.activation(dst, src, COPY)
+        query_mx = quantize("query", query_bf)
+        gout_bf = tile("gout_bf", [P, Q, PACK], BF16)
+        nc.vector.tensor_copy(*weave_views(gout_raw, gout_bf, 0, Q))
+        gout_mx = quantize("gout", gout_bf)
+
+        neg_lse = tile("neg_lse", [P, Q_TILES], F32)
+        nc.gpsimd.tensor_scalar(out=neg_lse[:], in0=lse_cols[:], scalar1=-1.0, scalar2=0.0, op0=MULT, op1=ADD)
+        fs_bank = bank("fs_bank", "bank_fs", [P, PACK, P])
+        for t in range(PACK):
+            nc.tensor.transpose(fs_bank[:, t, :], fs_cols[:, t : t + 1].to_broadcast([P, P]), ident[:])
+
+        dt_bf = tile("dt_bf", [P, Q, PACK], BF16)
+        dt_words = dt_bf[:].rearrange("p c t -> p (c t)").bitcast(F32).rearrange("p (c u) -> p c u", u=2)
+
+        def score_tile(m):
+            cols = slice(m * P, (m + 1) * P)
+            b_sb = tile("b_sb%d" % m, [P, U], F32)
+            nc.scalar.copy(b_sb[:], b_banks[m][:])
+            k1 = tile("k1_%d" % m, [P, I], F32)
+            for h in range(2):
+                nc.scalar.activation(k1[:, h * HALF : (h + 1) * HALF],
+                                     b_sb[:].indirect(place_list[:, h * LIST_HALF : (h + 1) * LIST_HALF]), COPY, bias=1.0)
+            a_bank = bank("a_bank%d" % m, "bank_a%d" % m, [P, I])
+            product(a_bank[:], query_mx, cols, keys_mx, FP4X4)
+            dp_bank = bank("dp_bank%d" % m, "bank_dp%d" % m, [P, I])
+            product(dp_bank[:], gout_mx, cols, vals_mx, FP4X4)
+            logits = tile("logits%d" % m, [P, I], F32)
+            nc.vector.tensor_tensor(out=logits[:], in0=a_bank[:], in1=k1[:], op=MULT)
+            weights = tile("weights%d" % m, [P, I], F32)
+            nc.scalar.activation(weights[:], logits[:], EXP, bias=neg_lse[:, m : m + 1])
+            grad = tile("grad%d" % m, [P, I], F32)
+            nc.vector.scalar_tensor_tensor(out=grad[:], in0=dp_bank[:], scalar=delta_cols[:, m : m + 1], in1=k1[:], op0=SUB, op1=MULT)
+            scaled = tile("scaled%d" % m, [P, I], F32)
+            nc.vector.tensor_tensor(out=scaled[:].rearrange("p (n t) -> p n t", t=PACK), in0=grad[:].rearrange("p (n t) -> p n t", t=PACK),
+                                    in1=fs_bank[:].rearrange("p t n -> p n t"), op=MULT)
+            ds = tile("ds%d" % m, [P, I], BF16)
+            nc.vector.tensor_tensor(out=ds[:], in0=weights[:], in1=scaled[:], op=MULT)
+            turned = bank("ds_turned%d" % m, "bank_a%d" % m, [P, 2, P])
+            turn_words(turned, ds[:])
+            nc.scalar.copy(dt_words[:, cols, :], turned[:].rearrange("p u c -> p c u"))
+
+        def key_plane(j, engines, tag):
+            picked = tile("keyrow_picked%d" % j, [P, I], BF16)
+            pieces = len(engines)
+            for h, engine in enumerate(engines):
+                n = I // pieces
+                dst = picked[:, h * n : (h + 1) * n]
+                src = keyrow_pool[j][:].indirect(slot_list[:, h * n // 16 : (h + 1) * n // 16])
+                if engine == "scalar":
+                    nc.scalar.activation(dst, src, COPY)
+                else:
+                    nc.vector.tensor_copy(out=dst, in_=src)
+            turned = bank("kt_turned%d" % j, tag, [P, 2, P])
+            turn_words(turned, picked[:])
+            kt_bf = tile("kt_bf%d" % j, [P, P, PACK], BF16)
+            kt_words = kt_bf[:].rearrange("p c t -> p (c t)").bitcast(F32).rearrange("p (c u) -> p c u", u=2)
+            nc.scalar.copy(kt_words, turned[:].rearrange("p u c -> p c u"))
+            return quantize("kt%d" % j, kt_bf)
+
+        score_tile(0)
+        score_tile(1)
+        kt_mx = [key_plane(0, ["scalar"], "bank_b0"), key_plane(1, ["scalar"], "bank_b1")]
+        dt_mx = quantize("dt", dt_bf)
+        kt_mx.append(key_plane(2, ["vector"], "bank_kt"))
+        kt_mx.append(key_plane(3, ["scalar", "vector"], "bank_b0"))
+
+        y = tile("y", [P, PACK, Q], F32)
+        out_planes = out_0.rearrange("(p j) q -> p j q", j=PACK)
+        for j, tag in enumerate(["bank_dp0", "bank_dp1", "bank_fs", "bank_a0"]):
+            gq_bank = bank("gq_bank%d" % j, tag, [P, Q])
+            product(gq_bank[:], kt_mx[j], slice(0, P), dt_mx, FP8X4)
+            nc.vector.tensor_tensor(out=y[:, j, :], in0=gq_bank[:], in1=res_raw[:, j, :], op=ADD)
+            nc.sync.dma_start(out=out_planes[:, j, :], in_=y[:, j, :])
+
+        y_bf = tile("y_bf", [P, Q, PACK], BF16)
+        nc.vector.tensor_copy(*weave_views(y, y_bf, 0, Q))
+        y_codes, y_scales = quantize("y", y_bf)
+        nc.sync.dma_start(out=out_1[0].rearrange("p c r -> p (c r)").bitcast(I32), in_=y_codes[:].bitcast(I32))
+        for quad in range(4):
+            queue = nc.scalar if quad % 2 else nc.sync
+            queue.dma_start(out=out_2[0, 4 * quad : 4 * quad + 4, :].bitcast(I32), in_=y_scales[32 * quad : 32 * quad + 4, :].bitcast(I32))

@@ -26,6 +26,7 @@ LINE = 4
 Q_TILES = Q // P
 HALF = I // 2
 LIST_HALF = HALF // 16
+SCALAR_SHARE = 96
 
 
 def weave_views(raw, grouped, c0, c1):
@@ -41,8 +42,8 @@ def tile_attend_gscaledquery_pl_kernel(tc, query, keys_words, keys_scales, pquer
         sb = ctx.enter_context(tc.tile_pool(name="sb", bufs=1))
         ps = ctx.enter_context(tc.psum_pool(name="ps", bufs=1))
 
-        def tile(name, shape, dtype):
-            return sb.tile(shape, dtype, name=name, align_bytes=64)
+        def tile(name, shape, dtype, tag=None):
+            return sb.tile(shape, dtype, name=name, tag=tag or name, align_bytes=64)
 
         def bank(name, tag, shape):
             return ps.tile(shape, F32, name=name, tag=tag)
@@ -52,31 +53,43 @@ def tile_attend_gscaledquery_pl_kernel(tc, query, keys_words, keys_scales, pquer
             nc.sync.dma_start(out=raw[:], in_=src.rearrange("(p t) w -> p t w", t=PACK))
             return raw
 
-        def load_packed(name, words, scales, zeroed):
-            pool_words = tile(name + "_words", [P, T], U16)
+        def load_words(name, words):
+            pool_words = tile(name + "_word_pool", [P, T], U16)
             nc.sync.dma_start(out=pool_words[:].bitcast(I32), in_=words[0].bitcast(I32))
-            for quad in range(4):
-                nc.sync.dma_start(out=zeroed[32 * quad : 32 * quad + 4, :].bitcast(I32),
-                                  in_=scales[0, 4 * quad : 4 * quad + 4, :].bitcast(I32))
             return pool_words
 
-        def gather_packed(name, pool_words, pool_scales):
-            words = tile(name + "_picked_words", [P, I], U16)
-            scales = tile(name + "_picked_scales", [P, I], U8)
-            nc.vector.tensor_copy(out=words[:], in_=pool_words[:].indirect(slot_list[:]))
-            nc.vector.tensor_copy(out=scales[:], in_=pool_scales[:].indirect(slot_list[:]))
-            return words, scales
+        def load_scales(queue, scales, zeroed):
+            for quad in range(4):
+                queue.dma_start(out=zeroed[32 * quad : 32 * quad + 4, :].bitcast(I32),
+                                  in_=scales[0, 4 * quad : 4 * quad + 4, :].bitcast(I32))
 
-        def quantize(name, grouped):
+        def gather_packed(name, pool, dtype, tag=None):
+            picked = tile(name, [P, I], dtype, tag)
+            nc.vector.tensor_copy(out=picked[:], in_=pool[:].indirect(slot_list[:]))
+            return picked[:]
+
+        def weave(raw, grouped, scalar_cols):
+            width = raw.shape[2]
+            if scalar_cols:
+                dst, src = weave_views(raw, grouped, 0, scalar_cols)
+                nc.scalar.activation(dst, src, COPY)
+            if scalar_cols < width:
+                nc.vector.tensor_copy(*weave_views(raw, grouped, scalar_cols, width))
+
+        def quantize(name, grouped, codes=None):
             width = grouped.shape[1]
-            codes = tile(name + "_codes", [P, width], U32)
+            if codes is None:
+                codes = tile(name + "_codes", [P, width], U32)[:]
             scales = tile(name + "_scales", [P, width], U8)
-            nc.vector.quantize_mx(out=codes[:].bitcast(FP8X4), scales=scales[:], in_=grouped[:].rearrange("p c t -> p (c t)"))
-            return codes, scales
+            nc.vector.quantize_mx(out=codes.bitcast(FP8X4), scales=scales[:], in_=grouped.rearrange("p c t -> p (c t)"))
+            return codes, scales[:]
 
         def product(out, stationary, cols, moving, moving_dtype):
             nc.tensor.matmul_mx(out=out, lhsT=stationary[0][:, cols].bitcast(FP8X4), lhsT_scale=stationary[1][:, cols],
-                                rhs=moving[0][:].bitcast(moving_dtype), rhs_scale=moving[1][:], start=True, stop=True)
+                                rhs=moving[0].bitcast(moving_dtype), rhs_scale=moving[1], start=True, stop=True)
+
+        def q_cols(m):
+            return slice(m * P, (m + 1) * P)
 
         def turn_words(dst, rows):
             words = rows.bitcast(F32)
@@ -87,25 +100,27 @@ def tile_attend_gscaledquery_pl_kernel(tc, query, keys_words, keys_scales, pquer
         val_scale_pool = tile("val_scale_pool", [P, T], U8)
         nc.vector.memset(key_scale_pool[:].bitcast(I32), 0)
         nc.vector.memset(val_scale_pool[:].bitcast(I32), 0)
+        fs_cols = tile("fs_cols", [P, PACK], F32)
+        nc.gpsimd.dma_start(out=fs_cols[:], in_=fs.rearrange("o (p t) -> p (o t)", t=PACK))
         ident = tile("ident", [P, P], F32)
         make_identity(nc, ident[:])
-
-        slot_list = tile("slot_list", [P, I // 16], U16)
-        nc.sync.dma_start(slot_list[:], offs)
-        key_word_pool = load_packed("key", keys_words, keys_scales, key_scale_pool)
-        pquery_raw = load_rows("pquery_raw", pquery)
-        place_raw = load_rows("place_raw", place)
-        place_list = tile("place_list", [P, I // 16], U16)
-        nc.sync.dma_start(place_list[:], offs2)
-        val_word_pool = load_packed("val", vals_words, vals_scales, val_scale_pool)
-        query_raw = load_rows("query_raw", query)
         lse_cols = tile("lse_cols", [P, Q_TILES], F32)
         delta_cols = tile("delta_cols", [P, Q_TILES], F32)
         with nc.allow_non_contiguous_dma(reason="one value a query row, on the row's partition"):
-            nc.sync.dma_start(out=lse_cols[:], in_=lse.rearrange("(m p) o -> p (m o)", p=P))
-            nc.sync.dma_start(out=delta_cols[:], in_=delta.rearrange("(m p) o -> p (m o)", p=P))
-        fs_cols = tile("fs_cols", [P, PACK], F32)
-        nc.sync.dma_start(out=fs_cols[:], in_=fs.rearrange("o (p t) -> p (o t)", t=PACK))
+            nc.gpsimd.dma_start(out=lse_cols[:], in_=lse.rearrange("(m p) o -> p (m o)", p=P))
+            nc.gpsimd.dma_start(out=delta_cols[:], in_=delta.rearrange("(m p) o -> p (m o)", p=P))
+
+        slot_list = tile("slot_list", [P, I // 16], U16)
+        nc.sync.dma_start(slot_list[:], offs)
+        pquery_raw = load_rows("pquery_raw", pquery)
+        load_scales(nc.sync, keys_scales, key_scale_pool)
+        place_raw = [load_rows("place_raw%d" % h, place[:, h * Q : (h + 1) * Q]) for h in range(2)]
+        query_raw = load_rows("query_raw", query)
+        load_scales(nc.sync, vals_scales, val_scale_pool)
+        place_list = tile("place_list", [P, I // 16], U16)
+        nc.sync.dma_start(place_list[:], offs2)
+        key_word_pool = load_words("key", keys_words)
+        val_word_pool = load_words("val", vals_words)
         gout_raw = load_rows("gout_raw", gout)
         keyrow_planes = keyrows.rearrange("(p j) t -> j p t", j=PACK)
         keyrow_pool = []
@@ -115,94 +130,129 @@ def tile_attend_gscaledquery_pl_kernel(tc, query, keys_words, keys_scales, pquer
             keyrow_pool.append(plane)
         res_raw = load_rows("res_raw", res)
 
-        keys_mx = gather_packed("key", key_word_pool, key_scale_pool)
-
         pquery_bf = tile("pquery_bf", [P, Q, PACK], BF16)
-        nc.vector.tensor_copy(*weave_views(pquery_raw, pquery_bf, 0, Q))
-        pquery_mx = quantize("pquery", pquery_bf)
-        place_bf = tile("place_bf", [P, U, PACK], BF16)
-        split = 192
-        dst, src = weave_views(place_raw, place_bf, 0, split)
-        nc.scalar.activation(dst, src, COPY)
-        nc.vector.tensor_copy(*weave_views(place_raw, place_bf, split, U))
-        place_mx = quantize("place", place_bf)
+        weave(pquery_raw, pquery_bf, 0)
+        pquery_mx = quantize("pquery", pquery_bf[:])
+        key_scales = gather_packed("key_scales", key_scale_pool, U8)
+        b_banks = [bank("b_bank%d" % m, "bank_b%d" % m, [P, U]) for m in range(Q_TILES)]
+        for h, scalar_cols in enumerate([Q, SCALAR_SHARE]):
+            place_bf = tile("place_bf%d" % h, [P, Q, PACK], BF16)
+            weave(place_raw[h], place_bf, scalar_cols)
+            place_mx = quantize("place%d" % h, place_bf[:])
+            for m in range(Q_TILES):
+                product(b_banks[m][:, h * Q : (h + 1) * Q], pquery_mx, q_cols(m), place_mx, FP8X4)
 
-        b_banks = []
-        for m in range(Q_TILES):
-            b_bank = bank("b_bank%d" % m, "bank_b%d" % m, [P, U])
-            product(b_bank[:], pquery_mx, slice(m * P, (m + 1) * P), place_mx, FP8X4)
-            b_banks.append(b_bank)
-
-        vals_mx = gather_packed("val", val_word_pool, val_scale_pool)
-
+        val_scales = gather_packed("val_scales", val_scale_pool, U8, "place_bf1")
         query_bf = tile("query_bf", [P, Q, PACK], BF16)
-        dst, src = weave_views(query_raw, query_bf, 0, Q)
-        nc.scalar.activation(dst, src, COPY)
-        query_mx = quantize("query", query_bf)
-        gout_bf = tile("gout_bf", [P, Q, PACK], BF16)
-        nc.vector.tensor_copy(*weave_views(gout_raw, gout_bf, 0, Q))
-        gout_mx = quantize("gout", gout_bf)
+        weave(query_raw, query_bf, Q)
+        query_mx = quantize("query", query_bf[:], tile("query_codes", [P, Q], U32, "val_scale_pool")[:])
+        keys_mx = (gather_packed("key_words", key_word_pool, U16), key_scales)
+        vals_mx = (gather_packed("val_words", val_word_pool, U16), val_scales)
 
-        neg_lse = tile("neg_lse", [P, Q_TILES], F32)
-        nc.gpsimd.tensor_scalar(out=neg_lse[:], in0=lse_cols[:], scalar1=-1.0, scalar2=0.0, op0=MULT, op1=ADD)
-        fs_bank = bank("fs_bank", "bank_fs", [P, PACK, P])
-        for t in range(PACK):
-            nc.tensor.transpose(fs_bank[:, t, :], fs_cols[:, t : t + 1].to_broadcast([P, P]), ident[:])
-
-        dt_bf = tile("dt_bf", [P, Q, PACK], BF16)
-        dt_words = dt_bf[:].rearrange("p c t -> p (c t)").bitcast(F32).rearrange("p (c u) -> p c u", u=2)
-
-        def score_tile(m):
-            cols = slice(m * P, (m + 1) * P)
-            b_sb = tile("b_sb%d" % m, [P, U], F32)
+        def look_up(m, tag):
+            b_sb = tile("b_sb%d" % m, [P, U], F32, tag)
             nc.scalar.copy(b_sb[:], b_banks[m][:])
             k1 = tile("k1_%d" % m, [P, I], F32)
             for h in range(2):
                 nc.scalar.activation(k1[:, h * HALF : (h + 1) * HALF],
                                      b_sb[:].indirect(place_list[:, h * LIST_HALF : (h + 1) * LIST_HALF]), COPY, bias=1.0)
-            a_bank = bank("a_bank%d" % m, "bank_a%d" % m, [P, I])
-            product(a_bank[:], query_mx, cols, keys_mx, FP4X4)
-            dp_bank = bank("dp_bank%d" % m, "bank_dp%d" % m, [P, I])
-            product(dp_bank[:], gout_mx, cols, vals_mx, FP4X4)
-            logits = tile("logits%d" % m, [P, I], F32)
-            nc.vector.tensor_tensor(out=logits[:], in0=a_bank[:], in1=k1[:], op=MULT)
-            weights = tile("weights%d" % m, [P, I], F32)
-            nc.scalar.activation(weights[:], logits[:], EXP, bias=neg_lse[:, m : m + 1])
-            grad = tile("grad%d" % m, [P, I], F32)
-            nc.vector.scalar_tensor_tensor(out=grad[:], in0=dp_bank[:], scalar=delta_cols[:, m : m + 1], in1=k1[:], op0=SUB, op1=MULT)
-            scaled = tile("scaled%d" % m, [P, I], F32)
-            nc.vector.tensor_tensor(out=scaled[:].rearrange("p (n t) -> p n t", t=PACK), in0=grad[:].rearrange("p (n t) -> p n t", t=PACK),
-                                    in1=fs_bank[:].rearrange("p t n -> p n t"), op=MULT)
-            ds = tile("ds%d" % m, [P, I], BF16)
-            nc.vector.tensor_tensor(out=ds[:], in0=weights[:], in1=scaled[:], op=MULT)
-            turned = bank("ds_turned%d" % m, "bank_a%d" % m, [P, 2, P])
-            turn_words(turned, ds[:])
-            nc.scalar.copy(dt_words[:, cols, :], turned[:].rearrange("p u c -> p c u"))
+            return k1
 
-        def key_plane(j, engines, tag):
+        k1s = [look_up(0, "query_raw"), look_up(1, None)]
+
+        neg_lse = tile("neg_lse", [P, Q_TILES], F32)
+        nc.gpsimd.tensor_scalar(out=neg_lse[:], in0=lse_cols[:], scalar1=-1.0, scalar2=0.0, op0=MULT, op1=ADD)
+        a_banks = []
+        for m in range(Q_TILES):
+            a_bank = bank("a_bank%d" % m, "bank_a%d" % m, [P, I])
+            product(a_bank[:], query_mx, q_cols(m), keys_mx, FP4X4)
+            a_banks.append(a_bank)
+        fs_bank = bank("fs_bank", "bank_fs", [P, PACK, P])
+        for t in range(PACK):
+            nc.tensor.transpose(fs_bank[:, t, :], fs_cols[:, t : t + 1].to_broadcast([P, P]), ident[:])
+
+        gout_bf = tile("gout_bf", [P, Q, PACK], BF16)
+        weave(gout_raw, gout_bf, 0)
+        logits = tile("logits", [P, Q_TILES * I], F32, "gout_raw")
+        scaled = tile("scaled", [P, Q_TILES * I], F32, "val_word_pool")
+
+        def slots(m):
+            return slice(m * I, (m + 1) * I)
+
+        def softmax_weights(m, tag):
+            nc.vector.tensor_tensor(out=logits[:, slots(m)], in0=a_banks[m][:], in1=k1s[m][:], op=MULT)
+            weights = tile("weights%d" % m, [P, I], F32, tag)
+            nc.scalar.activation(weights[:], logits[:, slots(m)], EXP, bias=neg_lse[:, m : m + 1])
+            return weights
+
+        def slot_scaled(m):
+            nc.vector.tensor_tensor(out=scaled[:, slots(m)].rearrange("p (n t) -> p n t", t=PACK), in0=k1s[m][:].rearrange("p (n t) -> p n t", t=PACK),
+                                    in1=fs_bank[:].rearrange("p t n -> p n t"), op=MULT)
+
+        def gradient(m):
+            dp_bank = bank("dp_bank%d" % m, "bank_dp%d" % m, [P, I])
+            product(dp_bank[:], gout_mx, q_cols(m), vals_mx, FP4X4)
+            grad = tile("grad%d" % m, [P, I], F32)
+            nc.vector.scalar_tensor_tensor(out=grad[:], in0=dp_bank[:], scalar=delta_cols[:, m : m + 1], in1=scaled[:, slots(m)], op0=SUB, op1=MULT)
+            return grad
+
+        def pick_rows(j, engines):
             picked = tile("keyrow_picked%d" % j, [P, I], BF16)
-            pieces = len(engines)
+            n = I // len(engines)
             for h, engine in enumerate(engines):
-                n = I // pieces
                 dst = picked[:, h * n : (h + 1) * n]
                 src = keyrow_pool[j][:].indirect(slot_list[:, h * n // 16 : (h + 1) * n // 16])
                 if engine == "scalar":
                     nc.scalar.activation(dst, src, COPY)
                 else:
                     nc.vector.tensor_copy(out=dst, in_=src)
-            turned = bank("kt_turned%d" % j, tag, [P, 2, P])
-            turn_words(turned, picked[:])
-            kt_bf = tile("kt_bf%d" % j, [P, P, PACK], BF16)
-            kt_words = kt_bf[:].rearrange("p c t -> p (c t)").bitcast(F32).rearrange("p (c u) -> p c u", u=2)
-            nc.scalar.copy(kt_words, turned[:].rearrange("p u c -> p c u"))
-            return quantize("kt%d" % j, kt_bf)
+            return picked
 
-        score_tile(0)
-        score_tile(1)
-        kt_mx = [key_plane(0, ["scalar"], "bank_b0"), key_plane(1, ["scalar"], "bank_b1")]
-        dt_mx = quantize("dt", dt_bf)
-        kt_mx.append(key_plane(2, ["vector"], "bank_kt"))
-        kt_mx.append(key_plane(3, ["scalar", "vector"], "bank_b0"))
+        def turn(name, tag, rows):
+            turned = bank(name, tag, [P, 2, P])
+            turn_words(turned, rows[:])
+            return turned
+
+        def copy_turned(grouped, turned):
+            words = grouped.rearrange("p c t -> p (c t)").bitcast(F32).rearrange("p (c u) -> p c u", u=2)
+            nc.scalar.copy(words, turned[:].rearrange("p u c -> p c u"))
+
+        weights = [softmax_weights(0, None)]
+        gout_mx = quantize("gout", gout_bf[:])
+        slot_scaled(0)
+        picked = [pick_rows(0, ["scalar"])]
+        weights.append(softmax_weights(1, "keyrow_pool0"))
+        slot_scaled(1)
+        picked.append(pick_rows(1, ["scalar"]))
+        grads = [gradient(m) for m in range(Q_TILES)]
+        ds = []
+        for m in range(Q_TILES):
+            ds_m = tile("ds%d" % m, [P, I], BF16)
+            nc.vector.tensor_tensor(out=ds_m[:], in0=weights[m][:], in1=grads[m][:], op=MULT)
+            ds.append(ds_m)
+        picked.append(pick_rows(2, ["vector"]))
+
+        early_bf = tile("early_bf", [P, (2 * P + Q) * PACK], BF16, "keyrow_pool1")
+        early = early_bf[:].rearrange("p (c t) -> p c t", t=PACK)
+        kt_bf = [early[:, 0:P, :], early[:, P : 2 * P, :]]
+        dt_bf = early[:, 2 * P :, :]
+        copy_turned(kt_bf[0], turn("kt_turned0", "bank_b0", picked[0]))
+        copy_turned(dt_bf[:, q_cols(0), :], turn("ds_turned0", "bank_a0", ds[0]))
+        copy_turned(kt_bf[1], turn("kt_turned1", "bank_b1", picked[1]))
+        copy_turned(dt_bf[:, q_cols(1), :], turn("ds_turned1", "bank_a1", ds[1]))
+        turned2 = turn("kt_turned2", "bank_kt", picked[2])
+
+        early_codes = tile("early_codes", [P, 2 * P + Q], U32, "keyrow_pool2")
+        kt01_codes, kt01_scales = quantize("kt01", early[:, : 2 * P, :], early_codes[:, : 2 * P])
+        kt_mx = [(kt01_codes[:, q_cols(j)], kt01_scales[:, q_cols(j)]) for j in range(2)]
+        dt_mx = quantize("dt", dt_bf, early_codes[:, 2 * P :])
+
+        picked.append(pick_rows(3, ["scalar", "vector"]))
+        turned3 = turn("kt_turned3", "bank_b0", picked[3])
+        for j, turned, tag in [(2, turned2, "keyrow_pool3"), (3, turned3, None)]:
+            late_bf = tile("kt_bf%d" % j, [P, P, PACK], BF16, tag)
+            copy_turned(late_bf[:], turned)
+            kt_mx.append(quantize("kt%d" % j, late_bf[:]))
 
         y = tile("y", [P, PACK, Q], F32)
         out_planes = out_0.rearrange("(p j) q -> p j q", j=PACK)
@@ -213,9 +263,9 @@ def tile_attend_gscaledquery_pl_kernel(tc, query, keys_words, keys_scales, pquer
             nc.sync.dma_start(out=out_planes[:, j, :], in_=y[:, j, :])
 
         y_bf = tile("y_bf", [P, Q, PACK], BF16)
-        nc.vector.tensor_copy(*weave_views(y, y_bf, 0, Q))
-        y_codes, y_scales = quantize("y", y_bf)
-        nc.sync.dma_start(out=out_1[0].rearrange("p c r -> p (c r)").bitcast(I32), in_=y_codes[:].bitcast(I32))
+        weave(y, y_bf, SCALAR_SHARE)
+        y_codes, y_scales = quantize("y", y_bf[:])
+        nc.sync.dma_start(out=out_1[0].rearrange("p c r -> p (c r)").bitcast(I32), in_=y_codes.bitcast(I32))
         for quad in range(4):
             queue = nc.scalar if quad % 2 else nc.sync
             queue.dma_start(out=out_2[0, 4 * quad : 4 * quad + 4, :].bitcast(I32), in_=y_scales[32 * quad : 32 * quad + 4, :].bitcast(I32))

@@ -59,9 +59,8 @@ def tile_attend_gscaledquery_pl_kernel(tc, query, keys_words, keys_scales, pquer
             return pool_words
 
         def load_scales(queue, scales, zeroed):
-            for quad in range(4):
-                queue.dma_start(out=zeroed[32 * quad : 32 * quad + 4, :].bitcast(I32),
-                                  in_=scales[0, 4 * quad : 4 * quad + 4, :].bitcast(I32))
+            for r in range(4):
+                queue.dma_start(out=zeroed[r:P:32, :].bitcast(I32), in_=scales[0, r:16:4, :].bitcast(I32))
 
         def gather_packed(name, pool, dtype, tag=None):
             picked = tile(name, [P, I], dtype, tag)
@@ -110,11 +109,11 @@ def tile_attend_gscaledquery_pl_kernel(tc, query, keys_words, keys_scales, pquer
             nc.gpsimd.dma_start(out=lse_cols[:], in_=lse.rearrange("(m p) o -> p (m o)", p=P))
             nc.gpsimd.dma_start(out=delta_cols[:], in_=delta.rearrange("(m p) o -> p (m o)", p=P))
 
+        pquery_raw = load_rows("pquery_raw", pquery)
         slot_list = tile("slot_list", [P, I // 16], U16)
         nc.sync.dma_start(slot_list[:], offs)
-        pquery_raw = load_rows("pquery_raw", pquery)
         load_scales(nc.sync, keys_scales, key_scale_pool)
-        place_raw = [load_rows("place_raw%d" % h, place[:, h * Q : (h + 1) * Q]) for h in range(2)]
+        place_raw = load_rows("place_raw", place)
         query_raw = load_rows("query_raw", query)
         load_scales(nc.sync, vals_scales, val_scale_pool)
         place_list = tile("place_list", [P, I // 16], U16)
@@ -135,14 +134,14 @@ def tile_attend_gscaledquery_pl_kernel(tc, query, keys_words, keys_scales, pquer
         pquery_mx = quantize("pquery", pquery_bf[:])
         key_scales = gather_packed("key_scales", key_scale_pool, U8)
         b_banks = [bank("b_bank%d" % m, "bank_b%d" % m, [P, U]) for m in range(Q_TILES)]
-        for h, scalar_cols in enumerate([Q, SCALAR_SHARE]):
+        for h in range(2):
             place_bf = tile("place_bf%d" % h, [P, Q, PACK], BF16)
-            weave(place_raw[h], place_bf, scalar_cols)
+            weave(place_raw[:, :, h * Q : (h + 1) * Q], place_bf, SCALAR_SHARE)
             place_mx = quantize("place%d" % h, place_bf[:])
             for m in range(Q_TILES):
                 product(b_banks[m][:, h * Q : (h + 1) * Q], pquery_mx, q_cols(m), place_mx, FP8X4)
 
-        val_scales = gather_packed("val_scales", val_scale_pool, U8, "place_bf1")
+        val_scales = gather_packed("val_scales", val_scale_pool, U8)
         query_bf = tile("query_bf", [P, Q, PACK], BF16)
         weave(query_raw, query_bf, Q)
         query_mx = quantize("query", query_bf[:], tile("query_codes", [P, Q], U32, "val_scale_pool")[:])
@@ -173,8 +172,9 @@ def tile_attend_gscaledquery_pl_kernel(tc, query, keys_words, keys_scales, pquer
 
         gout_bf = tile("gout_bf", [P, Q, PACK], BF16)
         weave(gout_raw, gout_bf, 0)
-        logits = tile("logits", [P, Q_TILES * I], F32, "gout_raw")
-        scaled = tile("scaled", [P, Q_TILES * I], F32, "val_word_pool")
+        products = tile("products", [P, 2 * Q_TILES * I], F32, "gout_raw")
+        logits = products[:, : Q_TILES * I]
+        scaled = products[:, Q_TILES * I :]
 
         def slots(m):
             return slice(m * I, (m + 1) * I)

@@ -18,7 +18,6 @@ COPY = mybir.ActivationFunctionType.Copy
 EXP = mybir.ActivationFunctionType.Exp
 MULT = mybir.AluOpType.mult
 ADD = mybir.AluOpType.add
-SUB = mybir.AluOpType.subtract
 
 P = 128
 PACK = 4
@@ -103,11 +102,8 @@ def tile_attend_gscaledquery_pl_kernel(tc, query, keys_words, keys_scales, pquer
         nc.gpsimd.dma_start(out=fs_cols[:], in_=fs.rearrange("o (p t) -> p (o t)", t=PACK))
         ident = tile("ident", [P, P], F32)
         make_identity(nc, ident[:])
-        lse_cols = tile("lse_cols", [P, Q_TILES], F32)
-        delta_cols = tile("delta_cols", [P, Q_TILES], F32)
-        with nc.allow_non_contiguous_dma(reason="one value a query row, on the row's partition"):
-            nc.gpsimd.dma_start(out=lse_cols[:], in_=lse.rearrange("(m p) o -> p (m o)", p=P))
-            nc.gpsimd.dma_start(out=delta_cols[:], in_=delta.rearrange("(m p) o -> p (m o)", p=P))
+        row_stats = tile("row_stats", [P, P], F32)
+        nc.gpsimd.memset(row_stats[:], 0.0)
 
         pquery_raw = load_rows("pquery_raw", pquery)
         slot_list = tile("slot_list", [P, I // 16], U16)
@@ -120,6 +116,8 @@ def tile_attend_gscaledquery_pl_kernel(tc, query, keys_words, keys_scales, pquer
         nc.sync.dma_start(place_list[:], offs2)
         key_word_pool = load_words("key", keys_words)
         val_word_pool = load_words("val", vals_words)
+        for first, stat in [(0, lse), (Q_TILES, delta)]:
+            nc.sync.dma_start(out=row_stats[first : first + Q_TILES, :], in_=stat.rearrange("(m p) o -> m (p o)", p=P))
         gout_raw = load_rows("gout_raw", gout)
         keyrow_planes = keyrows.rearrange("(p j) t -> j p t", j=PACK)
         keyrow_pool = []
@@ -159,13 +157,16 @@ def tile_attend_gscaledquery_pl_kernel(tc, query, keys_words, keys_scales, pquer
 
         k1s = [look_up(0, "query_raw"), look_up(1, None)]
 
-        neg_lse = tile("neg_lse", [P, Q_TILES], F32)
-        nc.gpsimd.tensor_scalar(out=neg_lse[:], in0=lse_cols[:], scalar1=-1.0, scalar2=0.0, op0=MULT, op1=ADD)
         a_banks = []
         for m in range(Q_TILES):
             a_bank = bank("a_bank%d" % m, "bank_a%d" % m, [P, I])
             product(a_bank[:], query_mx, q_cols(m), keys_mx, FP4X4)
             a_banks.append(a_bank)
+        stats_bank = bank("stats_bank", "bank_kt", [P, P])
+        nc.tensor.transpose(stats_bank[:], row_stats[:], ident[:])
+        neg_stats = tile("neg_stats", [P, 2 * Q_TILES], F32)
+        nc.scalar.activation(neg_stats[:], stats_bank[:, : 2 * Q_TILES], COPY, scale=-1.0)
+        neg_lse, neg_delta = neg_stats[:, :Q_TILES], neg_stats[:, Q_TILES:]
         fs_bank = bank("fs_bank", "bank_fs", [P, PACK, P])
         for t in range(PACK):
             nc.tensor.transpose(fs_bank[:, t, :], fs_cols[:, t : t + 1].to_broadcast([P, P]), ident[:])
@@ -193,7 +194,7 @@ def tile_attend_gscaledquery_pl_kernel(tc, query, keys_words, keys_scales, pquer
             dp_bank = bank("dp_bank%d" % m, "bank_dp%d" % m, [P, I])
             product(dp_bank[:], gout_mx, q_cols(m), vals_mx, FP4X4)
             grad = tile("grad%d" % m, [P, I], F32)
-            nc.vector.scalar_tensor_tensor(out=grad[:], in0=dp_bank[:], scalar=delta_cols[:, m : m + 1], in1=scaled[:, slots(m)], op0=SUB, op1=MULT)
+            nc.vector.scalar_tensor_tensor(out=grad[:], in0=dp_bank[:], scalar=neg_delta[:, m : m + 1], in1=scaled[:, slots(m)], op0=ADD, op1=MULT)
             return grad
 
         def pick_rows(j, engines):
@@ -263,7 +264,7 @@ def tile_attend_gscaledquery_pl_kernel(tc, query, keys_words, keys_scales, pquer
             nc.sync.dma_start(out=out_planes[:, j, :], in_=y[:, j, :])
 
         y_bf = tile("y_bf", [P, Q, PACK], BF16)
-        weave(y, y_bf, SCALAR_SHARE)
+        weave(y, y_bf, Q // 2)
         y_codes, y_scales = quantize("y", y_bf[:])
         nc.sync.dma_start(out=out_1[0].rearrange("p c r -> p (c r)").bitcast(I32), in_=y_codes.bitcast(I32))
         for quad in range(4):

@@ -22,16 +22,27 @@ ADD = mybir.AluOpType.add
 P = 128
 PACK = 4
 LINE = 4
+QUADRANT = 32
+SCALE_ROWS = 4
+LIST_ROWS = 16
 Q_TILES = Q // P
-HALF = I // 2
-LIST_HALF = HALF // 16
+PLACE_HALF = U // 2
 SCALAR_SHARE = 96
+KT_BF_BYTES = P * PACK * 2
 
 
-def weave_views(raw, grouped, c0, c1):
+def weave_views(raw, woven, c0, c1):
     src = raw[:, :, c0:c1].rearrange("p t (c i) -> p c t i", i=LINE)
-    dst = grouped[:, c0:c1, :].rearrange("p (c i) t -> p c t i", i=LINE)
+    dst = woven[:, c0:c1, :].rearrange("p (c i) t -> p c t i", i=LINE)
     return dst, src
+
+
+def q_cols(m):
+    return slice(m * P, (m + 1) * P)
+
+
+def slot_cols(m):
+    return slice(m * I, (m + 1) * I)
 
 
 def tile_attend_gscaledquery_pl_kernel(tc, query, keys_words, keys_scales, pquery, place, gout, vals_words, vals_scales,
@@ -39,6 +50,7 @@ def tile_attend_gscaledquery_pl_kernel(tc, query, keys_words, keys_scales, pquer
     nc = tc.nc
     with ExitStack() as ctx:
         sb = ctx.enter_context(tc.tile_pool(name="sb", bufs=1))
+        last = ctx.enter_context(tc.tile_pool(name="last", bufs=1))
         ps = ctx.enter_context(tc.psum_pool(name="ps", bufs=1))
 
         def tile(name, shape, dtype, tag=None):
@@ -53,46 +65,52 @@ def tile_attend_gscaledquery_pl_kernel(tc, query, keys_words, keys_scales, pquer
             return raw
 
         def load_words(name, words):
-            pool_words = tile(name + "_word_pool", [P, T], U16)
-            nc.sync.dma_start(out=pool_words[:].bitcast(I32), in_=words[0].bitcast(I32))
-            return pool_words
+            pool = tile(name, [P, T], U16)
+            nc.sync.dma_start(out=pool[:].bitcast(I32), in_=words[0].bitcast(I32))
+            return pool
 
-        def load_scales(queue, scales, zeroed):
-            for r in range(4):
-                queue.dma_start(out=zeroed[r:P:32, :].bitcast(I32), in_=scales[0, r:16:4, :].bitcast(I32))
+        def load_scales(scales, zeroed):
+            for r in range(SCALE_ROWS):
+                nc.sync.dma_start(out=zeroed[r:P:QUADRANT, :].bitcast(I32), in_=scales[0, r::SCALE_ROWS, :].bitcast(I32))
 
-        def gather_packed(name, pool, dtype, tag=None):
-            picked = tile(name, [P, I], dtype, tag)
+        def gather_packed(name, pool, dtype):
+            picked = tile(name, [P, I], dtype)
             nc.vector.tensor_copy(out=picked[:], in_=pool[:].indirect(slot_list[:]))
             return picked[:]
 
-        def weave(raw, grouped, scalar_cols):
+        def weave(raw, woven, scalar_cols):
             width = raw.shape[2]
             if scalar_cols:
-                dst, src = weave_views(raw, grouped, 0, scalar_cols)
+                dst, src = weave_views(raw, woven, 0, scalar_cols)
                 nc.scalar.activation(dst, src, COPY)
             if scalar_cols < width:
-                nc.vector.tensor_copy(*weave_views(raw, grouped, scalar_cols, width))
+                nc.vector.tensor_copy(*weave_views(raw, woven, scalar_cols, width))
 
-        def quantize(name, grouped, codes=None):
-            width = grouped.shape[1]
+        def quantize(name, woven, codes=None):
+            width = woven.shape[1]
             if codes is None:
                 codes = tile(name + "_codes", [P, width], U32)[:]
             scales = tile(name + "_scales", [P, width], U8)
-            nc.vector.quantize_mx(out=codes.bitcast(FP8X4), scales=scales[:], in_=grouped.rearrange("p c t -> p (c t)"))
+            nc.vector.quantize_mx(out=codes.bitcast(FP8X4), scales=scales[:], in_=woven.rearrange("p c t -> p (c t)"))
             return codes, scales[:]
 
-        def product(out, stationary, cols, moving, moving_dtype):
-            nc.tensor.matmul_mx(out=out, lhsT=stationary[0][:, cols].bitcast(FP8X4), lhsT_scale=stationary[1][:, cols],
+        def columns(operand, cols):
+            return operand[0][:, cols], operand[1][:, cols]
+
+        def product(out, stationary, moving, moving_dtype):
+            nc.tensor.matmul_mx(out=out, lhsT=stationary[0].bitcast(FP8X4), lhsT_scale=stationary[1],
                                 rhs=moving[0].bitcast(moving_dtype), rhs_scale=moving[1], start=True, stop=True)
 
-        def q_cols(m):
-            return slice(m * P, (m + 1) * P)
-
-        def turn_words(dst, rows):
-            words = rows.bitcast(F32)
+        def turn(name, tag, rows):
+            turned = bank(name, tag, [P, 2, P])
+            words = rows[:].bitcast(F32)
             for u in range(2):
-                nc.tensor.transpose(dst[:, u, :], words[:, u::2], ident[:])
+                nc.tensor.transpose(turned[:, u, :], words[:, u::2], ident[:])
+            return turned
+
+        def copy_turned(woven, turned):
+            words = woven.rearrange("p c t -> p (c t)").bitcast(F32).rearrange("p (c u) -> p c u", u=2)
+            nc.scalar.copy(words, turned[:].rearrange("p u c -> p c u"))
 
         key_scale_pool = tile("key_scale_pool", [P, T], U8)
         val_scale_pool = tile("val_scale_pool", [P, T], U8)
@@ -106,38 +124,42 @@ def tile_attend_gscaledquery_pl_kernel(tc, query, keys_words, keys_scales, pquer
         nc.gpsimd.memset(row_stats[:], 0.0)
 
         pquery_raw = load_rows("pquery_raw", pquery)
-        slot_list = tile("slot_list", [P, I // 16], U16)
+        slot_list = tile("slot_list", [P, I // LIST_ROWS], U16)
         nc.sync.dma_start(slot_list[:], offs)
-        load_scales(nc.sync, keys_scales, key_scale_pool)
+        load_scales(keys_scales, key_scale_pool)
         place_raw = load_rows("place_raw", place)
         query_raw = load_rows("query_raw", query)
-        load_scales(nc.sync, vals_scales, val_scale_pool)
-        place_list = tile("place_list", [P, I // 16], U16)
+        load_scales(vals_scales, val_scale_pool)
+        place_list = tile("place_list", [P, I // LIST_ROWS], U16)
         nc.sync.dma_start(place_list[:], offs2)
-        key_word_pool = load_words("key", keys_words)
-        val_word_pool = load_words("val", vals_words)
+        key_word_pool = load_words("key_word_pool", keys_words)
+        val_word_pool = load_words("val_word_pool", vals_words)
         for first, stat in [(0, lse), (Q_TILES, delta)]:
             nc.sync.dma_start(out=row_stats[first : first + Q_TILES, :], in_=stat.rearrange("(m p) o -> m (p o)", p=P))
         gout_raw = load_rows("gout_raw", gout)
         keyrow_planes = keyrows.rearrange("(p j) t -> j p t", j=PACK)
         keyrow_pool = []
         for j in range(PACK):
-            plane = tile("keyrow_pool%d" % j, [P, T], F32)
+            if j == PACK - 1:
+                plane = last.tile([P, T], F32, name="keyrow_pool3", align_bytes=64, offset=0)
+            else:
+                plane = tile("keyrow_pool%d" % j, [P, T], F32)
             nc.sync.dma_start(out=plane[:], in_=keyrow_planes[j])
             keyrow_pool.append(plane)
         res_raw = load_rows("res_raw", res)
 
         pquery_bf = tile("pquery_bf", [P, Q, PACK], BF16)
-        weave(pquery_raw, pquery_bf, 0)
-        pquery_mx = quantize("pquery", pquery_bf[:])
+        weave(pquery_raw, pquery_bf, Q)
         key_scales = gather_packed("key_scales", key_scale_pool, U8)
+        pquery_mx = quantize("pquery", pquery_bf[:], tile("pquery_codes", [P, Q], U32, "key_scale_pool")[:])
         b_banks = [bank("b_bank%d" % m, "bank_b%d" % m, [P, U]) for m in range(Q_TILES)]
-        for h in range(2):
-            place_bf = tile("place_bf%d" % h, [P, Q, PACK], BF16)
-            weave(place_raw[:, :, h * Q : (h + 1) * Q], place_bf, SCALAR_SHARE)
+        for h in range(U // PLACE_HALF):
+            places = slice(h * PLACE_HALF, (h + 1) * PLACE_HALF)
+            place_bf = tile("place_bf%d" % h, [P, PLACE_HALF, PACK], BF16)
+            weave(place_raw[:, :, places], place_bf, SCALAR_SHARE)
             place_mx = quantize("place%d" % h, place_bf[:])
             for m in range(Q_TILES):
-                product(b_banks[m][:, h * Q : (h + 1) * Q], pquery_mx, q_cols(m), place_mx, FP8X4)
+                product(b_banks[m][:, places], columns(pquery_mx, q_cols(m)), place_mx, FP8X4)
 
         val_scales = gather_packed("val_scales", val_scale_pool, U8)
         query_bf = tile("query_bf", [P, Q, PACK], BF16)
@@ -149,18 +171,19 @@ def tile_attend_gscaledquery_pl_kernel(tc, query, keys_words, keys_scales, pquer
         def look_up(m, tag):
             b_sb = tile("b_sb%d" % m, [P, U], F32, tag)
             nc.scalar.copy(b_sb[:], b_banks[m][:])
-            k1 = tile("k1_%d" % m, [P, I], F32)
+            k1_tile = tile("k1_%d" % m, [P, I], F32)
+            n = I // 2
             for h in range(2):
-                nc.scalar.activation(k1[:, h * HALF : (h + 1) * HALF],
-                                     b_sb[:].indirect(place_list[:, h * LIST_HALF : (h + 1) * LIST_HALF]), COPY, bias=1.0)
-            return k1
+                offsets = place_list[:, h * n // LIST_ROWS : (h + 1) * n // LIST_ROWS]
+                nc.scalar.activation(k1_tile[:, h * n : (h + 1) * n], b_sb[:].indirect(offsets), COPY, bias=1.0)
+            return k1_tile
 
-        k1s = [look_up(0, "query_raw"), look_up(1, None)]
+        k1 = [look_up(0, "query_raw"), look_up(1, None)]
 
         a_banks = []
         for m in range(Q_TILES):
             a_bank = bank("a_bank%d" % m, "bank_a%d" % m, [P, I])
-            product(a_bank[:], query_mx, q_cols(m), keys_mx, FP4X4)
+            product(a_bank[:], columns(query_mx, q_cols(m)), keys_mx, FP4X4)
             a_banks.append(a_bank)
         stats_bank = bank("stats_bank", "bank_kt", [P, P])
         nc.tensor.transpose(stats_bank[:], row_stats[:], ident[:])
@@ -175,98 +198,92 @@ def tile_attend_gscaledquery_pl_kernel(tc, query, keys_words, keys_scales, pquer
         weave(gout_raw, gout_bf, 0)
         products = tile("products", [P, 2 * Q_TILES * I], F32, "gout_raw")
         logits = products[:, : Q_TILES * I]
-        scaled = products[:, Q_TILES * I :]
-
-        def slots(m):
-            return slice(m * I, (m + 1) * I)
+        k1_fs = products[:, Q_TILES * I :]
 
         def softmax_weights(m, tag):
-            nc.vector.tensor_tensor(out=logits[:, slots(m)], in0=a_banks[m][:], in1=k1s[m][:], op=MULT)
-            weights = tile("weights%d" % m, [P, I], F32, tag)
-            nc.scalar.activation(weights[:], logits[:, slots(m)], EXP, bias=neg_lse[:, m : m + 1])
-            return weights
+            nc.vector.tensor_tensor(out=logits[:, slot_cols(m)], in0=a_banks[m][:], in1=k1[m][:], op=MULT)
+            weights_tile = tile("weights%d" % m, [P, I], F32, tag)
+            nc.scalar.activation(weights_tile[:], logits[:, slot_cols(m)], EXP, bias=neg_lse[:, m : m + 1])
+            return weights_tile
 
-        def slot_scaled(m):
-            nc.vector.tensor_tensor(out=scaled[:, slots(m)].rearrange("p (n t) -> p n t", t=PACK), in0=k1s[m][:].rearrange("p (n t) -> p n t", t=PACK),
+        def scale_slots(m):
+            nc.vector.tensor_tensor(out=k1_fs[:, slot_cols(m)].rearrange("p (n t) -> p n t", t=PACK),
+                                    in0=k1[m][:].rearrange("p (n t) -> p n t", t=PACK),
                                     in1=fs_bank[:].rearrange("p t n -> p n t"), op=MULT)
 
         def gradient(m):
             dp_bank = bank("dp_bank%d" % m, "bank_dp%d" % m, [P, I])
-            product(dp_bank[:], gout_mx, q_cols(m), vals_mx, FP4X4)
+            product(dp_bank[:], columns(gout_mx, q_cols(m)), vals_mx, FP4X4)
             grad = tile("grad%d" % m, [P, I], F32)
-            nc.vector.scalar_tensor_tensor(out=grad[:], in0=dp_bank[:], scalar=neg_delta[:, m : m + 1], in1=scaled[:, slots(m)], op0=ADD, op1=MULT)
+            nc.vector.scalar_tensor_tensor(out=grad[:], in0=dp_bank[:], scalar=neg_delta[:, m : m + 1],
+                                           in1=k1_fs[:, slot_cols(m)], op0=ADD, op1=MULT)
             return grad
 
         def pick_rows(j, engines):
-            picked = tile("keyrow_picked%d" % j, [P, I], BF16)
+            picked_tile = tile("keyrow_picked%d" % j, [P, I], BF16)
             n = I // len(engines)
             for h, engine in enumerate(engines):
-                dst = picked[:, h * n : (h + 1) * n]
-                src = keyrow_pool[j][:].indirect(slot_list[:, h * n // 16 : (h + 1) * n // 16])
+                dst = picked_tile[:, h * n : (h + 1) * n]
+                src = keyrow_pool[j][:].indirect(slot_list[:, h * n // LIST_ROWS : (h + 1) * n // LIST_ROWS])
                 if engine == "scalar":
                     nc.scalar.activation(dst, src, COPY)
                 else:
                     nc.vector.tensor_copy(out=dst, in_=src)
-            return picked
-
-        def turn(name, tag, rows):
-            turned = bank(name, tag, [P, 2, P])
-            turn_words(turned, rows[:])
-            return turned
-
-        def copy_turned(grouped, turned):
-            words = grouped.rearrange("p c t -> p (c t)").bitcast(F32).rearrange("p (c u) -> p c u", u=2)
-            nc.scalar.copy(words, turned[:].rearrange("p u c -> p c u"))
+            return picked_tile
 
         weights = [softmax_weights(0, None)]
         gout_mx = quantize("gout", gout_bf[:])
-        slot_scaled(0)
+        scale_slots(0)
         picked = [pick_rows(0, ["scalar"])]
         weights.append(softmax_weights(1, "keyrow_pool0"))
-        slot_scaled(1)
+        scale_slots(1)
         picked.append(pick_rows(1, ["scalar"]))
         grads = [gradient(m) for m in range(Q_TILES)]
         ds = []
         for m in range(Q_TILES):
-            ds_m = tile("ds%d" % m, [P, I], BF16)
-            nc.vector.tensor_tensor(out=ds_m[:], in0=weights[m][:], in1=grads[m][:], op=MULT)
-            ds.append(ds_m)
+            ds_tile = tile("ds%d" % m, [P, I], BF16)
+            nc.vector.tensor_tensor(out=ds_tile[:], in0=weights[m][:], in1=grads[m][:], op=MULT)
+            ds.append(ds_tile)
         picked.append(pick_rows(2, ["vector"]))
 
         early_bf = tile("early_bf", [P, (2 * P + Q) * PACK], BF16, "keyrow_pool1")
         early = early_bf[:].rearrange("p (c t) -> p c t", t=PACK)
-        kt_bf = [early[:, 0:P, :], early[:, P : 2 * P, :]]
-        dt_bf = early[:, 2 * P :, :]
-        copy_turned(kt_bf[0], turn("kt_turned0", "bank_b0", picked[0]))
-        copy_turned(dt_bf[:, q_cols(0), :], turn("ds_turned0", "bank_a0", ds[0]))
-        copy_turned(kt_bf[1], turn("kt_turned1", "bank_b1", picked[1]))
-        copy_turned(dt_bf[:, q_cols(1), :], turn("ds_turned1", "bank_a1", ds[1]))
+        kt01_bf, dt_bf = early[:, : 2 * P, :], early[:, 2 * P :, :]
+        for m in range(Q_TILES):
+            copy_turned(kt01_bf[:, q_cols(m), :], turn("kt_turned%d" % m, "bank_b%d" % m, picked[m]))
+            copy_turned(dt_bf[:, q_cols(m), :], turn("ds_turned%d" % m, "bank_a%d" % m, ds[m]))
         turned2 = turn("kt_turned2", "bank_kt", picked[2])
-
-        early_codes = tile("early_codes", [P, 2 * P + Q], U32, "keyrow_pool2")
-        kt01_codes, kt01_scales = quantize("kt01", early[:, : 2 * P, :], early_codes[:, : 2 * P])
-        kt_mx = [(kt01_codes[:, q_cols(j)], kt01_scales[:, q_cols(j)]) for j in range(2)]
-        dt_mx = quantize("dt", dt_bf, early_codes[:, 2 * P :])
+        kt01_mx = quantize("kt01", kt01_bf, tile("kt01_codes", [P, 2 * P], U32, "keyrow_pool2")[:])
+        kt_mx = [columns(kt01_mx, q_cols(j)) for j in range(2)]
 
         picked.append(pick_rows(3, ["scalar", "vector"]))
         turned3 = turn("kt_turned3", "bank_b0", picked[3])
-        for j, turned, tag in [(2, turned2, "keyrow_pool3"), (3, turned3, None)]:
-            late_bf = tile("kt_bf%d" % j, [P, P, PACK], BF16, tag)
+        dt_mx = quantize("dt", dt_bf, last.tile([P, Q], U32, name="dt_codes", align_bytes=64, offset=0)[:])
+        for j, turned in [(2, turned2), (3, turned3)]:
+            late_bf = last.tile([P, P, PACK], BF16, name="kt_bf%d" % j, align_bytes=64, offset=KT_BF_BYTES * j)
             copy_turned(late_bf[:], turned)
             kt_mx.append(quantize("kt%d" % j, late_bf[:]))
 
         y = tile("y", [P, PACK, Q], F32)
         out_planes = out_0.rearrange("(p j) q -> p j q", j=PACK)
-        for j, tag in enumerate(["bank_dp0", "bank_dp1", "bank_fs", "bank_a0"]):
-            gq_bank = bank("gq_bank%d" % j, tag, [P, Q])
-            product(gq_bank[:], kt_mx[j], slice(0, P), dt_mx, FP8X4)
-            nc.vector.tensor_tensor(out=y[:, j, :], in0=gq_bank[:], in1=res_raw[:, j, :], op=ADD)
+        for j, tags in enumerate([["bank_dp0"], ["bank_dp1"], ["bank_fs"], ["bank_a0", "bank_a1"]]):
+            width = Q // len(tags)
+            for h, tag in enumerate(tags):
+                cols = slice(h * width, (h + 1) * width)
+                gq_bank = bank("gq_bank%d_%d" % (j, h), tag, [P, width])
+                product(gq_bank[:], kt_mx[j], columns(dt_mx, cols), FP8X4)
+                nc.vector.tensor_tensor(out=y[:, j, cols], in0=gq_bank[:], in1=res_raw[:, j, cols], op=ADD)
             nc.sync.dma_start(out=out_planes[:, j, :], in_=y[:, j, :])
 
         y_bf = tile("y_bf", [P, Q, PACK], BF16)
-        weave(y, y_bf, Q // 2)
-        y_codes, y_scales = quantize("y", y_bf[:])
-        nc.sync.dma_start(out=out_1[0].rearrange("p c r -> p (c r)").bitcast(I32), in_=y_codes.bitcast(I32))
-        for quad in range(4):
-            queue = nc.scalar if quad % 2 else nc.sync
-            queue.dma_start(out=out_2[0, 4 * quad : 4 * quad + 4, :].bitcast(I32), in_=y_scales[32 * quad : 32 * quad + 4, :].bitcast(I32))
+        weave(y, y_bf, P)
+        y_codes = tile("y_codes", [P, Q], U32)
+        y_scales = tile("y_scales", [P, Q], U8)
+        for m in reversed(range(Q_TILES)):
+            nc.vector.quantize_mx(out=y_codes[:, q_cols(m)].bitcast(FP8X4), scales=y_scales[:, q_cols(m)],
+                                  in_=y_bf[:, q_cols(m), :].rearrange("p c t -> p (c t)"))
+        nc.sync.dma_start(out=out_1[0].rearrange("p c r -> p (c r)").bitcast(I32), in_=y_codes[:].bitcast(I32))
+        for g in range(P // QUADRANT):
+            queue = nc.scalar if g % 2 else nc.sync
+            queue.dma_start(out=out_2[0, SCALE_ROWS * g : SCALE_ROWS * (g + 1), :].bitcast(I32),
+                            in_=y_scales[QUADRANT * g : QUADRANT * g + SCALE_ROWS, :].bitcast(I32))

from contextlib import ExitStack

import concourse.mybir as mybir
from concourse.masks import make_identity

D, E, T, I, Q, U = 512, 512, 2048, 512, 256, 512
FLOPS = 2 * Q * (D * I + D * U + E * I + I * D)

F32 = mybir.dt.float32
BF16 = mybir.dt.bfloat16
I32 = mybir.dt.int32
U32 = mybir.dt.uint32
U16 = mybir.dt.uint16
U8 = mybir.dt.uint8
FP8X4 = mybir.dt.float8_e4m3fn_x4
FP4X4 = mybir.dt.float4_e2m1fn_x4
COPY = mybir.ActivationFunctionType.Copy
EXP = mybir.ActivationFunctionType.Exp
MULT = mybir.AluOpType.mult
ADD = mybir.AluOpType.add

P = 128
PACK = 4
LINE = 4
QUADRANT = 32
SCALE_ROWS = 4
LIST_ROWS = 16
Q_TILES = Q // P
PLACE_HALF = U // 2
SCALAR_SHARE = 96
KT_BF_BYTES = P * PACK * 2


def weave_views(raw, woven, c0, c1):
    src = raw[:, :, c0:c1].rearrange("p t (c i) -> p c t i", i=LINE)
    dst = woven[:, c0:c1, :].rearrange("p (c i) t -> p c t i", i=LINE)
    return dst, src


def q_cols(m):
    return slice(m * P, (m + 1) * P)


def slot_cols(m):
    return slice(m * I, (m + 1) * I)


def tile_attend_gscaledquery_pl_kernel(tc, query, keys_words, keys_scales, pquery, place, gout, vals_words, vals_scales,
                                        lse, delta, fs, keyrows, res, offs, offs2, out_0, out_1, out_2):
    nc = tc.nc
    with ExitStack() as ctx:
        sb = ctx.enter_context(tc.tile_pool(name="sb", bufs=1))
        last = ctx.enter_context(tc.tile_pool(name="last", bufs=1))
        ps = ctx.enter_context(tc.psum_pool(name="ps", bufs=1))

        def tile(name, shape, dtype, tag=None):
            return sb.tile(shape, dtype, name=name, tag=tag or name, align_bytes=64)

        def bank(name, tag, shape):
            return ps.tile(shape, F32, name=name, tag=tag)

        def load_rows(name, src):
            raw = tile(name, [P, PACK, src.shape[1]], F32)
            nc.sync.dma_start(out=raw[:], in_=src.rearrange("(p t) w -> p t w", t=PACK))
            return raw

        def load_words(name, words):
            pool = tile(name, [P, T], U16)
            nc.sync.dma_start(out=pool[:].bitcast(I32), in_=words[0].bitcast(I32))
            return pool

        def load_scales(scales, zeroed):
            for r in range(SCALE_ROWS):
                nc.sync.dma_start(out=zeroed[r:P:QUADRANT, :].bitcast(I32), in_=scales[0, r::SCALE_ROWS, :].bitcast(I32))

        def gather_packed(name, pool, dtype):
            picked = tile(name, [P, I], dtype)
            nc.vector.tensor_copy(out=picked[:], in_=pool[:].indirect(slot_list[:]))
            return picked[:]

        def weave(raw, woven, scalar_cols):
            width = raw.shape[2]
            if scalar_cols:
                dst, src = weave_views(raw, woven, 0, scalar_cols)
                nc.scalar.activation(dst, src, COPY)
            if scalar_cols < width:
                nc.vector.tensor_copy(*weave_views(raw, woven, scalar_cols, width))

        def quantize(name, woven, codes=None):
            width = woven.shape[1]
            if codes is None:
                codes = tile(name + "_codes", [P, width], U32)[:]
            scales = tile(name + "_scales", [P, width], U8)
            nc.vector.quantize_mx(out=codes.bitcast(FP8X4), scales=scales[:], in_=woven.rearrange("p c t -> p (c t)"))
            return codes, scales[:]

        def columns(operand, cols):
            return operand[0][:, cols], operand[1][:, cols]

        def product(out, stationary, moving, moving_dtype):
            nc.tensor.matmul_mx(out=out, lhsT=stationary[0].bitcast(FP8X4), lhsT_scale=stationary[1],
                                rhs=moving[0].bitcast(moving_dtype), rhs_scale=moving[1], start=True, stop=True)

        def turn(name, tag, rows):
            turned = bank(name, tag, [P, 2, P])
            words = rows[:].bitcast(F32)
            for u in range(2):
                nc.tensor.transpose(turned[:, u, :], words[:, u::2], ident[:])
            return turned

        def copy_turned(woven, turned):
            words = woven.rearrange("p c t -> p (c t)").bitcast(F32).rearrange("p (c u) -> p c u", u=2)
            nc.scalar.copy(words, turned[:].rearrange("p u c -> p c u"))

        key_scale_pool = tile("key_scale_pool", [P, T], U8)
        val_scale_pool = tile("val_scale_pool", [P, T], U8)
        nc.vector.memset(key_scale_pool[:].bitcast(I32), 0)
        nc.vector.memset(val_scale_pool[:].bitcast(I32), 0)
        fs_cols = tile("fs_cols", [P, PACK], F32)
        nc.gpsimd.dma_start(out=fs_cols[:], in_=fs.rearrange("o (p t) -> p (o t)", t=PACK))
        ident = tile("ident", [P, P], F32)
        make_identity(nc, ident[:])
        row_stats = tile("row_stats", [P, P], F32)
        nc.gpsimd.memset(row_stats[:], 0.0)

        pquery_raw = load_rows("pquery_raw", pquery)
        slot_list = tile("slot_list", [P, I // LIST_ROWS], U16)
        nc.sync.dma_start(slot_list[:], offs)
        load_scales(keys_scales, key_scale_pool)
        place_raw = load_rows("place_raw", place)
        query_raw = load_rows("query_raw", query)
        load_scales(vals_scales, val_scale_pool)
        place_list = tile("place_list", [P, I // LIST_ROWS], U16)
        nc.sync.dma_start(place_list[:], offs2)
        key_word_pool = load_words("key_word_pool", keys_words)
        val_word_pool = load_words("val_word_pool", vals_words)
        for first, stat in [(0, lse), (Q_TILES, delta)]:
            nc.sync.dma_start(out=row_stats[first : first + Q_TILES, :], in_=stat.rearrange("(m p) o -> m (p o)", p=P))
        gout_raw = load_rows("gout_raw", gout)
        keyrow_planes = keyrows.rearrange("(p j) t -> j p t", j=PACK)
        keyrow_pool = []
        for j in range(PACK):
            if j == PACK - 1:
                plane = last.tile([P, T], F32, name="keyrow_pool3", align_bytes=64, offset=0)
            else:
                plane = tile("keyrow_pool%d" % j, [P, T], F32)
            nc.sync.dma_start(out=plane[:], in_=keyrow_planes[j])
            keyrow_pool.append(plane)
        res_raw = load_rows("res_raw", res)

        pquery_bf = tile("pquery_bf", [P, Q, PACK], BF16)
        weave(pquery_raw, pquery_bf, Q)
        key_scales = gather_packed("key_scales", key_scale_pool, U8)
        pquery_mx = quantize("pquery", pquery_bf[:], tile("pquery_codes", [P, Q], U32, "key_scale_pool")[:])
        b_banks = [bank("b_bank%d" % m, "bank_b%d" % m, [P, U]) for m in range(Q_TILES)]
        for h in range(U // PLACE_HALF):
            places = slice(h * PLACE_HALF, (h + 1) * PLACE_HALF)
            place_bf = tile("place_bf%d" % h, [P, PLACE_HALF, PACK], BF16)
            weave(place_raw[:, :, places], place_bf, SCALAR_SHARE)
            place_mx = quantize("place%d" % h, place_bf[:])
            for m in range(Q_TILES):
                product(b_banks[m][:, places], columns(pquery_mx, q_cols(m)), place_mx, FP8X4)

        val_scales = gather_packed("val_scales", val_scale_pool, U8)
        query_bf = tile("query_bf", [P, Q, PACK], BF16)
        weave(query_raw, query_bf, Q)
        query_mx = quantize("query", query_bf[:], tile("query_codes", [P, Q], U32, "val_scale_pool")[:])
        keys_mx = (gather_packed("key_words", key_word_pool, U16), key_scales)
        vals_mx = (gather_packed("val_words", val_word_pool, U16), val_scales)

        def look_up(m, tag):
            b_sb = tile("b_sb%d" % m, [P, U], F32, tag)
            nc.scalar.copy(b_sb[:], b_banks[m][:])
            k1_tile = tile("k1_%d" % m, [P, I], F32)
            n = I // 2
            for h in range(2):
                offsets = place_list[:, h * n // LIST_ROWS : (h + 1) * n // LIST_ROWS]
                nc.scalar.activation(k1_tile[:, h * n : (h + 1) * n], b_sb[:].indirect(offsets), COPY, bias=1.0)
            return k1_tile

        k1 = [look_up(0, "query_raw"), look_up(1, None)]

        a_banks = []
        for m in range(Q_TILES):
            a_bank = bank("a_bank%d" % m, "bank_a%d" % m, [P, I])
            product(a_bank[:], columns(query_mx, q_cols(m)), keys_mx, FP4X4)
            a_banks.append(a_bank)
        stats_bank = bank("stats_bank", "bank_kt", [P, P])
        nc.tensor.transpose(stats_bank[:], row_stats[:], ident[:])
        neg_stats = tile("neg_stats", [P, 2 * Q_TILES], F32)
        nc.scalar.activation(neg_stats[:], stats_bank[:, : 2 * Q_TILES], COPY, scale=-1.0)
        neg_lse, neg_delta = neg_stats[:, :Q_TILES], neg_stats[:, Q_TILES:]
        fs_bank = bank("fs_bank", "bank_fs", [P, PACK, P])
        for t in range(PACK):
            nc.tensor.transpose(fs_bank[:, t, :], fs_cols[:, t : t + 1].to_broadcast([P, P]), ident[:])

        gout_bf = tile("gout_bf", [P, Q, PACK], BF16)
        weave(gout_raw, gout_bf, 0)
        products = tile("products", [P, 2 * Q_TILES * I], F32, "gout_raw")
        logits = products[:, : Q_TILES * I]
        k1_fs = products[:, Q_TILES * I :]

        def softmax_weights(m, tag):
            nc.vector.tensor_tensor(out=logits[:, slot_cols(m)], in0=a_banks[m][:], in1=k1[m][:], op=MULT)
            weights_tile = tile("weights%d" % m, [P, I], F32, tag)
            nc.scalar.activation(weights_tile[:], logits[:, slot_cols(m)], EXP, bias=neg_lse[:, m : m + 1])
            return weights_tile

        def scale_slots(m):
            nc.vector.tensor_tensor(out=k1_fs[:, slot_cols(m)].rearrange("p (n t) -> p n t", t=PACK),
                                    in0=k1[m][:].rearrange("p (n t) -> p n t", t=PACK),
                                    in1=fs_bank[:].rearrange("p t n -> p n t"), op=MULT)

        def gradient(m):
            dp_bank = bank("dp_bank%d" % m, "bank_dp%d" % m, [P, I])
            product(dp_bank[:], columns(gout_mx, q_cols(m)), vals_mx, FP4X4)
            grad = tile("grad%d" % m, [P, I], F32)
            nc.vector.scalar_tensor_tensor(out=grad[:], in0=dp_bank[:], scalar=neg_delta[:, m : m + 1],
                                           in1=k1_fs[:, slot_cols(m)], op0=ADD, op1=MULT)
            return grad

        def pick_rows(j, engines):
            picked_tile = tile("keyrow_picked%d" % j, [P, I], BF16)
            n = I // len(engines)
            for h, engine in enumerate(engines):
                dst = picked_tile[:, h * n : (h + 1) * n]
                src = keyrow_pool[j][:].indirect(slot_list[:, h * n // LIST_ROWS : (h + 1) * n // LIST_ROWS])
                if engine == "scalar":
                    nc.scalar.activation(dst, src, COPY)
                else:
                    nc.vector.tensor_copy(out=dst, in_=src)
            return picked_tile

        weights = [softmax_weights(0, None)]
        gout_mx = quantize("gout", gout_bf[:])
        scale_slots(0)
        picked = [pick_rows(0, ["scalar"])]
        weights.append(softmax_weights(1, "keyrow_pool0"))
        scale_slots(1)
        picked.append(pick_rows(1, ["scalar"]))
        grads = [gradient(m) for m in range(Q_TILES)]
        ds = []
        for m in range(Q_TILES):
            ds_tile = tile("ds%d" % m, [P, I], BF16)
            nc.vector.tensor_tensor(out=ds_tile[:], in0=weights[m][:], in1=grads[m][:], op=MULT)
            ds.append(ds_tile)
        picked.append(pick_rows(2, ["vector"]))

        early_bf = tile("early_bf", [P, (2 * P + Q) * PACK], BF16, "keyrow_pool1")
        early = early_bf[:].rearrange("p (c t) -> p c t", t=PACK)
        kt01_bf, dt_bf = early[:, : 2 * P, :], early[:, 2 * P :, :]
        for m in range(Q_TILES):
            copy_turned(kt01_bf[:, q_cols(m), :], turn("kt_turned%d" % m, "bank_b%d" % m, picked[m]))
            copy_turned(dt_bf[:, q_cols(m), :], turn("ds_turned%d" % m, "bank_a%d" % m, ds[m]))
        turned2 = turn("kt_turned2", "bank_kt", picked[2])
        kt01_mx = quantize("kt01", kt01_bf, tile("kt01_codes", [P, 2 * P], U32, "keyrow_pool2")[:])
        kt_mx = [columns(kt01_mx, q_cols(j)) for j in range(2)]

        picked.append(pick_rows(3, ["scalar", "vector"]))
        turned3 = turn("kt_turned3", "bank_b0", picked[3])
        dt_mx = quantize("dt", dt_bf, last.tile([P, Q], U32, name="dt_codes", align_bytes=64, offset=0)[:])
        for j, turned in [(2, turned2), (3, turned3)]:
            late_bf = last.tile([P, P, PACK], BF16, name="kt_bf%d" % j, align_bytes=64, offset=KT_BF_BYTES * j)
            copy_turned(late_bf[:], turned)
            kt_mx.append(quantize("kt%d" % j, late_bf[:]))

        y = tile("y", [P, PACK, Q], F32)
        out_planes = out_0.rearrange("(p j) q -> p j q", j=PACK)
        for j, tags in enumerate([["bank_dp0"], ["bank_dp1"], ["bank_fs"], ["bank_a0", "bank_a1"]]):
            width = Q // len(tags)
            for h, tag in enumerate(tags):
                cols = slice(h * width, (h + 1) * width)
                gq_bank = bank("gq_bank%d_%d" % (j, h), tag, [P, width])
                product(gq_bank[:], kt_mx[j], columns(dt_mx, cols), FP8X4)
                nc.vector.tensor_tensor(out=y[:, j, cols], in0=gq_bank[:], in1=res_raw[:, j, cols], op=ADD)
            nc.sync.dma_start(out=out_planes[:, j, :], in_=y[:, j, :])

        y_bf = tile("y_bf", [P, Q, PACK], BF16)
        weave(y, y_bf, P)
        y_codes = tile("y_codes", [P, Q], U32)
        y_scales = tile("y_scales", [P, Q], U8)
        for m in reversed(range(Q_TILES)):
            nc.vector.quantize_mx(out=y_codes[:, q_cols(m)].bitcast(FP8X4), scales=y_scales[:, q_cols(m)],
                                  in_=y_bf[:, q_cols(m), :].rearrange("p c t -> p (c t)"))
        nc.sync.dma_start(out=out_1[0].rearrange("p c r -> p (c r)").bitcast(I32), in_=y_codes[:].bitcast(I32))
        for g in range(P // QUADRANT):
            queue = nc.scalar if g % 2 else nc.sync
            queue.dma_start(out=out_2[0, SCALE_ROWS * g : SCALE_ROWS * (g + 1), :].bitcast(I32),
                            in_=y_scales[QUADRANT * g : QUADRANT * g + SCALE_ROWS, :].bitcast(I32))
